import numpy as np
import ml_dtypes


def mxq(x, axis, fmt="e4m3"):
    dtype, down = {"e4m3": (ml_dtypes.float8_e4m3fn, 7), "e5m2": (ml_dtypes.float8_e5m2, 14)}[fmt]
    v = np.moveaxis(np.asarray(x, np.float32).astype(ml_dtypes.bfloat16).astype(np.float64), axis, -1)
    blocks = v.reshape(v.shape[:-1] + (-1, 32))
    amax = np.abs(blocks).max(-1, keepdims=True)
    byte = np.maximum(np.where(amax > 0, np.frexp(amax)[1] - 1 + 127, 0) - down, 1)
    scale = np.exp2(byte - 127.0)
    codes = (blocks / scale).astype(np.float32).astype(dtype).astype(np.float64)
    return np.moveaxis((codes * scale).reshape(v.shape), -1, axis)


WIDE = False


def mx_kscale(k):
    if not WIDE:
        return np.ones(k)
    levels = np.array([10, -10, 5, -5, 0])
    if k % 512:
        return np.exp2(np.random.permutation(np.resize(levels, k // 32))).repeat(32)
    a = np.empty((k // 512, 16))
    for p in range(k // 512):
        a[p, :8] = np.random.permutation(np.resize(levels, 8))
        for g in range(8):
            far = levels[np.abs(levels - a[p, g]) >= 10]
            a[p, g + 8] = far[np.random.randint(len(far))]
    return np.exp2(a.ravel()).repeat(32)


BF16 = ml_dtypes.bfloat16


def bf(x):
    return np.asarray(x, np.float32).astype(BF16)


def f64(x):
    return np.asarray(x).astype(np.float64)


N, K, P, H = 128, 4096, 2048, 2048


def draw0():
    s = mx_kscale(K)
    r = mx_kscale(P)
    t = mx_kscale(P)
    return {
        "z": bf(np.random.standard_normal((N, K)) * s),
        "m": bf(np.random.standard_normal((N, P)) * r),
        "ez": bf(np.random.standard_normal(K) / np.sqrt(K) / s),
        "at": bf(np.random.standard_normal((P, P)) / np.sqrt(P) / r[:, None] * t),
        "bvec": bf(np.random.standard_normal(P) * 0.7 * t),
        "wz": bf(np.random.standard_normal((K, H)) * 0.7 / np.sqrt(K) / s[:, None]),
        "wm": bf(np.random.standard_normal((P, H)) * 0.7 / np.sqrt(P) / t[:, None]),
    }


def write_scalar(z, ez):
    return np.sum(z * ez[None, :], axis=-1)


def update_memory(m, u, at, bvec):
    a = mxq(m, 1, "e4m3") @ mxq(at, 0, "e4m3")
    return a + u[:, None] * bvec[None, :]


def core(z, m, ez, at, bvec, wz, wm):
    z, m = f64(z), f64(m)
    u = write_scalar(z, f64(ez))
    m_new = update_memory(m, u, f64(at), f64(bvec))
    s = (mxq(z, 1, "e4m3") @ mxq(f64(wz), 0, "e4m3")) + (mxq(m_new, 1, "e4m3") @ mxq(f64(wm), 0, "e4m3"))
    return np.tanh(s)


def e4m3fn_bytes(y):
    return np.clip(np.asarray(y, np.float64), -448.0, 448.0).astype(np.float32).astype(ml_dtypes.float8_e4m3fn).view(np.uint8)


def e4m3fn_values(b):
    return np.asarray(b, np.uint8).view(ml_dtypes.float8_e4m3fn).astype(np.float64)


def setup_inputs():
    d = draw0()
    x0 = np.asarray(d['wz']).astype(np.float64)
    s = (np.max(np.abs(x0), axis=(1,), keepdims=True) / 448.0).astype(np.float32)
    out = {}
    for k, v in d.items():
        if k == 'wz':
            out['wz_bytes'] = e4m3fn_bytes(x0 / s.astype(np.float64))
            out['wz_scale'] = s
        else:
            out[k] = v
    return out


def reference(z, m, ez, at, bvec, wz_bytes, wz_scale, wm):
    return core(z, m, ez, at, bvec, e4m3fn_values(wz_bytes) * wz_scale.astype(np.float64), wm)

@@ -1,0 +1,326 @@
+from contextlib import ExitStack
+
+import concourse.mybir as mybir
+from concourse.masks import make_identity
+
+TOK, K, MEM, H = 128, 4096, 2048, 2048
+FLOPS = 2 * TOK * (MEM * MEM + K * H + MEM * H + K + MEM)
+
+F32 = mybir.dt.float32
+BF16 = mybir.dt.bfloat16
+U32 = mybir.dt.uint32
+U8 = mybir.dt.uint8
+FP8 = mybir.dt.float8_e4m3fn
+FP8X4 = mybir.dt.float8_e4m3fn_x4
+ACT = mybir.ActivationFunctionType
+ALU = mybir.AluOpType
+
+P = 128
+PACK = 4
+PASS = P * PACK
+CH = 512
+PAIR = 2 * CH
+STEPS = 32
+
+
+def tile_legendrememoryunitstep_w_kernel(tc, z, m, ez, at, bvec, wz_bytes, wz_scale, wm, out):
+    nc = tc.nc
+    with ExitStack() as ctx:
+        keep = ctx.enter_context(tc.tile_pool(name="keep", bufs=1))
+        raw_pool = ctx.enter_context(tc.tile_pool(name="raw", bufs=4))
+        wide_pool = ctx.enter_context(tc.tile_pool(name="wide", bufs=3))
+        group_pool = ctx.enter_context(tc.tile_pool(name="group", bufs=3))
+        code_pool = ctx.enter_context(tc.tile_pool(name="code", bufs=7))
+        acc_pool = ctx.enter_context(tc.psum_pool(name="acc", bufs=1))
+        turn_pool = ctx.enter_context(tc.psum_pool(name="turn", bufs=2))
+
+        ident = keep.tile([P, P], F32, name="ident")
+        make_identity(nc, ident[:])
+        zero = keep.tile([P, 1], F32, name="zero")
+        nc.vector.memset(zero[:], 0.0)
+
+        scale_first = keep.tile([P, PACK], F32, name="scale_first")
+        scale_rest = keep.tile([P, 7, PACK], F32, name="scale_rest")
+        ez_sb = keep.tile([P, 8, PACK], BF16, name="ez_sb")
+        bvec_sb = keep.tile([P, MEM], BF16, name="bvec_sb")
+        z_sb = keep.tile([P, K], BF16, name="z_sb", align_bytes=64)
+        m_sb = keep.tile([P, MEM], BF16, name="m_sb", align_bytes=64)
+        z_group = keep.tile([P, 8, PASS], BF16, name="z_group", align_bytes=64)
+        z_codes = keep.tile([P, 8, TOK], U32, name="z_codes", align_bytes=64)
+        z_scales = keep.tile([P, 8, TOK], U8, name="z_scales", align_bytes=64)
+        m_group = keep.tile([P, 4, PASS], BF16, name="m_group", align_bytes=64)
+        m_codes = keep.tile([P, 4, TOK], U32, name="m_codes", align_bytes=64)
+        m_scales = keep.tile([P, 4, TOK], U8, name="m_scales", align_bytes=64)
+        new_sb = keep.tile([P, MEM], BF16, name="new_sb", align_bytes=64)
+        new_group = keep.tile([P, 4, PASS], BF16, name="new_group", align_bytes=64)
+        new_codes = keep.tile([P, 4, TOK], U32, name="new_codes", align_bytes=64)
+        new_scales = keep.tile([P, 4, TOK], U8, name="new_scales", align_bytes=64)
+        u_sb = keep.tile([P, 1], F32, name="u_sb")
+        warm = keep.tile([P, 1], F32, name="warm")
+
+        scale_view = wz_scale.rearrange("(g p t) o -> p g (t o)", p=P, t=PACK)
+        ez_view = ez.rearrange("(g p t) -> p g t", p=P, t=PACK)
+        at_view = at.rearrange("(g p t) n -> g p t n", p=P, t=PACK)
+        wm_view = wm.rearrange("(g p t) n -> g p t n", p=P, t=PACK)
+        wz_view = wz_bytes.rearrange("(g p t) n -> g p t n", p=P, t=PACK)
+
+        acc = [acc_pool.tile([P, CH], F32, name="acc%d" % c) for c in range(4)]
+
+        def plain_unit(i):
+            r = i % 16
+            return i // 16, (r % 8) // 2, 2 * (r // 8) + r % 2
+
+        vcopy = nc.vector.tensor_copy
+        scopy = nc.scalar.copy
+
+        raw = {}
+        codes_raw = {}
+        wide = {}
+        group_b = {}
+        group_z = {}
+        codes_b = {}
+        codes_z = {}
+        first = {}
+
+        def load_plain(j, parts=1):
+            which, g, c = plain_unit(2 * j)
+            view = (at_view, wm_view)[which]
+            t = raw_pool.tile([P, PACK, PAIR], BF16, name="raw_b", align_bytes=64)
+            raw[j] = t
+            w = PAIR // parts
+            return [
+                lambda k=k: nc.sync.dma_start(
+                    out=t[:, :, k * w : (k + 1) * w],
+                    in_=view[g][:, :, c * CH + k * w : c * CH + (k + 1) * w],
+                )
+                for k in range(parts)
+            ]
+
+        def load_bytes(j, parts=1):
+            g, c0 = j // 2, (j % 2) * PAIR
+            t = raw_pool.tile([P, PACK, PAIR], U8, name="raw_z", align_bytes=64)
+            codes_raw[j] = t
+            w = PAIR // parts
+            return [
+                lambda k=k: nc.sync.dma_start(
+                    out=t[:, :, k * w : (k + 1) * w],
+                    in_=wz_view[g][:, :, c0 + k * w : c0 + (k + 1) * w],
+                )
+                for k in range(parts)
+            ]
+
+        def scale_col(g, t):
+            return scale_first[:, t : t + 1] if g == 0 else scale_rest[:, g - 1, t : t + 1]
+
+        def widen(j, ts, a=0, b=PAIR):
+            if j not in wide:
+                wt = wide_pool.tile([P, PACK, PAIR], BF16, name="wide", align_bytes=64)
+                wide[j] = wt
+            for t in ts:
+                nc.scalar.activation(
+                    out=wide[j][:, t, a:b],
+                    in_=codes_raw[j][:, t, a:b].bitcast(FP8),
+                    func=ACT.Copy,
+                    scale=scale_col(j // 2, t),
+                )
+
+        def interleave(engine_copy, dst, src, a, b, off):
+            engine_copy(
+                out=dst[:, a:b, :].rearrange("p (c i) t -> p c t i", i=4),
+                in_=src[:, :, off + a : off + b].rearrange("p t (c i) -> p c t i", i=4),
+            )
+
+        def get_group(store, i, name):
+            if i not in store:
+                gt = group_pool.tile([P, CH, PACK], BF16, name=name, align_bytes=64)
+                store[i] = gt
+            return store[i]
+
+        def share_b(i, a, b, engine_copy):
+            if b > a:
+                interleave(engine_copy, get_group(group_b, i, "group_b"), raw[i // 2], a, b, (i % 2) * CH)
+
+        def share_z(i, a, b, engine_copy):
+            if b > a:
+                interleave(engine_copy, get_group(group_z, i, "group_z"), wide[i // 2], a, b, (i % 2) * CH)
+
+        def quantize(store, groups, i, name):
+            ct = code_pool.tile([P, CH], U32, name="codes_" + name, align_bytes=64)
+            st = code_pool.tile([P, CH], U8, name="scales_" + name, align_bytes=64)
+            store[i] = (ct, st)
+            nc.vector.quantize_mx(
+                out=ct[:].bitcast(FP8X4), scales=st[:], in_=groups[i][:].rearrange("p w j -> p (w j)")
+            )
+
+        def quantize_rows(codes, scales, group, g0, g1):
+            nc.vector.quantize_mx(
+                out=codes[:, g0:g1, :].rearrange("p g n -> p (g n)").bitcast(FP8X4),
+                scales=scales[:, g0:g1, :].rearrange("p g n -> p (g n)"),
+                in_=group[:, g0:g1, :].rearrange("p g k -> p (g k)"),
+            )
+
+        def mm(acc_ap, codes, scales, g, pair, start, stop):
+            ct, st = pair
+            nc.tensor.matmul_mx(
+                out=acc_ap,
+                lhsT=codes[:, g, :].bitcast(FP8X4),
+                lhsT_scale=scales[:, g, :],
+                rhs=ct[:].bitcast(FP8X4),
+                rhs_scale=st[:],
+                start=start,
+                stop=stop,
+            )
+
+        def mm_b(i):
+            which, g, c = plain_unit(i)
+            if which == 0:
+                if g == 0:
+                    ft = acc_pool.tile([P, CH], F32, name="first%d" % (c % 2))
+                    first[c] = ft
+                mm(first[c][:], m_codes, m_scales, g, codes_b[i], g == 0, g == 3)
+            else:
+                mm(acc[c][:], new_codes, new_scales, g, codes_b[i], False, False)
+
+        def mm_z(i):
+            g, c = i // 4, i % 4
+            mm(acc[c][:], z_codes, z_scales, g, codes_z[i], g == 0, g == 7)
+
+        turned = {}
+
+        def turn(key, src, g):
+            tt = turn_pool.tile([P, 2, 2, TOK], F32, name="turned")
+            turned[key] = tt
+            words = src[:].bitcast(F32)
+            for k in (0, 1):
+                for u in (0, 1):
+                    lo = 256 * (g + k)
+                    nc.tensor.transpose(tt[:, k, u, :], words[:, lo + u : lo + 256 : 2], ident[:])
+
+        def unturn(copy, key, group, g):
+            copy(
+                out=group[:, g : g + 2, :].bitcast(F32).rearrange("p g (r u) -> p g r u", u=2),
+                in_=turned[key][:].rearrange("p g u r -> p g r u"),
+            )
+
+        def turn_z(q):
+            turn("z%d" % q, z_sb, 2 * q)
+            unturn(vcopy, "z%d" % q, z_group, 2 * q)
+
+        def write_scalar(u_ps):
+            for g in range(8):
+                for t in range(PACK):
+                    nc.tensor.matmul(
+                        u_ps[:],
+                        lhsT=z_group[:, g, :].rearrange("p (n t) -> p n t", t=PACK)[:, :, t],
+                        rhs=ez_sb[:, g, t : t + 1],
+                        start=(g == 0 and t == 0),
+                        stop=(g == 7 and t == PACK - 1),
+                    )
+
+        def finish(c):
+            res = keep.tile([P, CH], F32, name="res%d" % c)
+            nc.scalar.activation(out=res[:], in_=acc[c][:], func=ACT.Tanh)
+            nc.sync.dma_start(out=out[:, c * CH : (c + 1) * CH], in_=res[:])
+
+        def add_write(c):
+            nc.vector.scalar_tensor_tensor(
+                out=new_sb[:, c * CH : (c + 1) * CH],
+                in0=bvec_sb[:, c * CH : (c + 1) * CH],
+                scalar=u_sb[:, 0:1],
+                in1=first[c][:],
+                op0=ALU.mult,
+                op1=ALU.add,
+            )
+
+        def scalar_cols(i):
+            return 0 if i < 4 else 192
+
+        def scalar_cols_z(i):
+            return 160 if i >= 30 else 0
+
+
+        with tc.manual_schedule():
+            nc.scalar.dma_start(out=scale_first[:], in_=scale_view[:, 0, :])
+            nc.scalar.activation(out=warm[:], in_=zero[:], func=ACT.Tanh)
+            lz = load_bytes(0, 2)
+            lb = load_plain(0, 2)
+            lz[0]()
+            lb[0]()
+            lz[1]()
+            nc.sync.dma_start(out=m_sb[:], in_=m)
+            lb[1]()
+            nc.sync.dma_start(out=z_sb[:, 0 : K // 2], in_=z[:, 0 : K // 2])
+            nc.sync.dma_start(out=z_sb[:, K // 2 : K], in_=z[:, K // 2 : K])
+            nc.scalar.dma_start(out=scale_rest[:], in_=scale_view[:, 1:8, :])
+            nc.scalar.dma_start(out=ez_sb[:], in_=ez_view)
+            load_bytes(1)[0]()
+            load_plain(1)[0]()
+            load_bytes(2)[0]()
+            load_plain(2)[0]()
+            nc.sync.dma_start(out=bvec_sb[:], in_=bvec.partition_broadcast(P))
+            load_bytes(3)[0]()
+
+            widen(0, range(4), 0, CH)
+            turn("m0", m_sb, 0)
+            turn("m1", m_sb, 2)
+            unturn(scopy, "m0", m_group, 0)
+            unturn(scopy, "m1", m_group, 2)
+            widen(0, range(4), CH, PAIR)
+
+            for i in range(STEPS):
+                if i % 2 == 0:
+                    j = i // 2
+                    if j + 3 < 16:
+                        load_plain(j + 3)[0]()
+                    if j + 4 < 16:
+                        load_bytes(j + 4)[0]()
+
+                if i + 1 < STEPS:
+                    share_b(i + 1, CH - scalar_cols(i + 1), CH, scopy)
+                jw = i // 2 + 1
+                if jw < 16:
+                    widen(jw, (0, 1) if i % 2 == 0 else (2, 3))
+                if i in (11, 19):
+                    unturn(scopy, "n%d" % i, new_group, 0 if i == 11 else 2)
+                if 29 <= i < STEPS - 1:
+                    share_z(i + 1, CH - scalar_cols_z(i + 1), CH, scopy)
+
+                share_b(i, 0, CH - scalar_cols(i), vcopy)
+                if i == 1:
+                    turn_z(0)
+                    turn_z(1)
+                if i == 2:
+                    quantize_rows(m_codes, m_scales, m_group, 0, 4)
+                if i == 3:
+                    quantize_rows(z_codes, z_scales, z_group, 0, 4)
+                if i == 4:
+                    quantize_rows(z_codes, z_scales, z_group, 4, 8)
+                    vcopy(out=u_sb[:], in_=u_ps[:])
+                if i in (12, 20):
+                    quantize_rows(new_codes, new_scales, new_group, (i - 12) // 4, (i - 12) // 4 + 2)
+                if i > 0:
+                    quantize(codes_z, group_z, i - 1, "z")
+                if i in (8, 9, 16, 17):
+                    add_write((0, 1, 2, 3)[(8, 9, 16, 17).index(i)])
+                share_z(i, 0, CH - scalar_cols_z(i), vcopy)
+                if i == 1:
+                    turn_z(2)
+                    turn_z(3)
+                    u_ps = turn_pool.tile([P, 1], F32, name="turned")
+                    write_scalar(u_ps)
+                quantize(codes_b, group_b, i, "b")
+                if i == STEPS - 1:
+                    quantize(codes_z, group_z, i, "z")
+
+                if i in (10, 18):
+                    turn("n%d" % (i + 1), new_sb, 0 if i == 10 else 2)
+                if i >= 4:
+                    for k in range(5) if i == 4 else (i,):
+                        if k > 0:
+                            mm_z(k - 1)
+                        mm_b(k)
+                if i == STEPS - 1:
+                    mm_z(i)
+                if i >= 29:
+                    finish(i - 29)
+            finish(3)

@@ -36,6 +36,8 @@ def tile_legendrememoryunitstep_w_kernel(tc, z, m, ez, at, bvec, wz_bytes, wz_sc
 
         ident = keep.tile([P, P], F32, name="ident")
         make_identity(nc, ident[:])
+        ident_b = keep.tile([P, P], BF16, name="ident_b")
+        nc.vector.tensor_copy(out=ident_b[:], in_=ident[:])
         zero = keep.tile([P, 1], F32, name="zero")
         nc.vector.memset(zero[:], 0.0)
 
@@ -73,6 +75,7 @@ def tile_legendrememoryunitstep_w_kernel(tc, z, m, ez, at, bvec, wz_bytes, wz_sc
         vcopy = nc.vector.tensor_copy
         scopy = nc.scalar.copy
 
+        woven = {}
         raw = {}
         codes_raw = {}
         wide = {}
@@ -82,49 +85,41 @@ def tile_legendrememoryunitstep_w_kernel(tc, z, m, ez, at, bvec, wz_bytes, wz_sc
         codes_z = {}
         first = {}
 
-        def load_plain(j, parts=1):
-            which, g, c = plain_unit(2 * j)
-            view = (at_view, wm_view)[which]
-            t = raw_pool.tile([P, PACK, PAIR], BF16, name="raw_b", align_bytes=64)
-            raw[j] = t
-            w = PAIR // parts
-            return [
-                lambda k=k: nc.sync.dma_start(
-                    out=t[:, :, k * w : (k + 1) * w],
-                    in_=view[g][:, :, c * CH + k * w : c * CH + (k + 1) * w],
-                )
-                for k in range(parts)
-            ]
+        def load_plain(i, n=2):
+            which, g, c = plain_unit(i)
+            pool = raw_pool if n == 2 else keep
+            t = pool.tile([P, PACK, n * CH], BF16, name="raw_b" if n == 2 else "raw_b%d" % i, align_bytes=64)
+            for k in range(n):
+                raw[i + k] = (t, k * CH)
+            nc.sync.dma_start(out=t[:], in_=(at_view, wm_view)[which][g][:, :, c * CH : (c + n) * CH])
 
-        def load_bytes(j, parts=1):
-            g, c0 = j // 2, (j % 2) * PAIR
-            t = raw_pool.tile([P, PACK, PAIR], U8, name="raw_z", align_bytes=64)
-            codes_raw[j] = t
-            w = PAIR // parts
-            return [
-                lambda k=k: nc.sync.dma_start(
-                    out=t[:, :, k * w : (k + 1) * w],
-                    in_=wz_view[g][:, :, c0 + k * w : c0 + (k + 1) * w],
-                )
-                for k in range(parts)
-            ]
+        def load_bytes(i, n=2):
+            g, c = i // 4, i % 4
+            pool = raw_pool if n == 2 else keep
+            t = pool.tile([P, PACK, n * CH], U8, name="raw_z" if n == 2 else "raw_z%d" % i, align_bytes=64)
+            for k in range(n):
+                codes_raw[i + k] = (t, k * CH)
+            nc.sync.dma_start(out=t[:], in_=wz_view[g][:, :, c * CH : (c + n) * CH])
 
         def scale_col(g, t):
             return scale_first[:, t : t + 1] if g == 0 else scale_rest[:, g - 1, t : t + 1]
 
-        def widen(j, ts, a=0, b=PAIR):
-            if j not in wide:
-                wt = wide_pool.tile([P, PACK, PAIR], BF16, name="wide", align_bytes=64)
-                wide[j] = wt
+        def widen(i, ts, n=2):
+            if i not in wide:
+                pool = wide_pool if n == 2 else keep
+                wt = pool.tile([P, PACK, n * CH], BF16, name="wide" if n == 2 else "wide%d" % i, align_bytes=64)
+                for k in range(n):
+                    wide[i + k] = (wt, k * CH)
             for t in ts:
                 nc.scalar.activation(
-                    out=wide[j][:, t, a:b],
-                    in_=codes_raw[j][:, t, a:b].bitcast(FP8),
+                    out=wide[i][0][:, t, :],
+                    in_=codes_raw[i][0][:, t, :].bitcast(FP8),
                     func=ACT.Copy,
-                    scale=scale_col(j // 2, t),
+                    scale=scale_col(i // 4, t),
                 )
 
-        def interleave(engine_copy, dst, src, a, b, off):
+        def interleave(engine_copy, dst, source, a, b):
+            src, off = source
             engine_copy(
                 out=dst[:, a:b, :].rearrange("p (c i) t -> p c t i", i=4),
                 in_=src[:, :, off + a : off + b].rearrange("p t (c i) -> p c t i", i=4),
@@ -138,11 +133,32 @@ def tile_legendrememoryunitstep_w_kernel(tc, z, m, ez, at, bvec, wz_bytes, wz_sc
 
         def share_b(i, a, b, engine_copy):
             if b > a:
-                interleave(engine_copy, get_group(group_b, i, "group_b"), raw[i // 2], a, b, (i % 2) * CH)
+                interleave(engine_copy, get_group(group_b, i, "group_b"), raw[i], a, b)
 
         def share_z(i, a, b, engine_copy):
             if b > a:
-                interleave(engine_copy, get_group(group_z, i, "group_z"), wide[i // 2], a, b, (i % 2) * CH)
+                interleave(engine_copy, get_group(group_z, i, "group_z"), wide[i], a, b)
+
+        def tensor_share_b(i):
+            src, off = raw[i]
+            it = turn_pool.tile([P, 2, CH], BF16, name="turned")
+            woven[i] = it
+            for k in (0, 1):
+                lo = off + CH // 2 + k * P
+                nc.tensor.matmul(
+                    it[:, k, :],
+                    lhsT=ident_b[:],
+                    rhs=src[:, :, lo : lo + P].rearrange("p t c -> p c t"),
+                    start=True,
+                    stop=True,
+                )
+
+        def fetch_share_b(i):
+            nc.scalar.copy(
+                out=get_group(group_b, i, "group_b")[:, CH // 2 :, :].rearrange("p c t -> p (c t)"),
+                in_=woven[i][:].rearrange("p k n -> p (k n)"),
+            )
+
 
         def quantize(store, groups, i, name):
             ct = code_pool.tile([P, CH], U32, name="codes_" + name, align_bytes=64)
@@ -233,7 +249,13 @@ def tile_legendrememoryunitstep_w_kernel(tc, z, m, ez, at, bvec, wz_bytes, wz_sc
             )
 
         def scalar_cols(i):
-            return 0 if i < 4 else 192
+            if i < 3:
+                return 0
+            if i == 3:
+                return 128
+            return 256 if i in by_tensor else 240
+
+        by_tensor = range(6, 29, 2)
 
         def scalar_cols_z(i):
             return 160 if i >= 30 else 0
@@ -242,44 +264,44 @@ def tile_legendrememoryunitstep_w_kernel(tc, z, m, ez, at, bvec, wz_bytes, wz_sc
         with tc.manual_schedule():
             nc.scalar.dma_start(out=scale_first[:], in_=scale_view[:, 0, :])
             nc.scalar.activation(out=warm[:], in_=zero[:], func=ACT.Tanh)
-            lz = load_bytes(0, 2)
-            lb = load_plain(0, 2)
-            lz[0]()
-            lb[0]()
-            lz[1]()
+            load_bytes(0, 1)
+            load_plain(0, 1)
+            load_bytes(1, 1)
             nc.sync.dma_start(out=m_sb[:], in_=m)
-            lb[1]()
+            load_plain(1, 1)
             nc.sync.dma_start(out=z_sb[:, 0 : K // 2], in_=z[:, 0 : K // 2])
             nc.sync.dma_start(out=z_sb[:, K // 2 : K], in_=z[:, K // 2 : K])
             nc.scalar.dma_start(out=scale_rest[:], in_=scale_view[:, 1:8, :])
             nc.scalar.dma_start(out=ez_sb[:], in_=ez_view)
-            load_bytes(1)[0]()
-            load_plain(1)[0]()
-            load_bytes(2)[0]()
-            load_plain(2)[0]()
+            load_bytes(2)
+            load_plain(2)
+            load_bytes(4)
+            load_plain(4)
             nc.sync.dma_start(out=bvec_sb[:], in_=bvec.partition_broadcast(P))
-            load_bytes(3)[0]()
+            load_bytes(6)
 
-            widen(0, range(4), 0, CH)
+            widen(0, range(4), 1)
             turn("m0", m_sb, 0)
             turn("m1", m_sb, 2)
             unturn(scopy, "m0", m_group, 0)
             unturn(scopy, "m1", m_group, 2)
-            widen(0, range(4), CH, PAIR)
+            widen(1, range(4), 1)
 
             for i in range(STEPS):
                 if i % 2 == 0:
-                    j = i // 2
-                    if j + 3 < 16:
-                        load_plain(j + 3)[0]()
-                    if j + 4 < 16:
-                        load_bytes(j + 4)[0]()
+                    if i + 6 < STEPS:
+                        load_plain(i + 6)
+                    if i + 8 < STEPS:
+                        load_bytes(i + 8)
 
-                if i + 1 < STEPS:
+                if i + 2 in by_tensor:
+                    tensor_share_b(i + 2)
+                if i + 1 in by_tensor:
+                    fetch_share_b(i + 1)
+                elif i + 1 < STEPS:
                     share_b(i + 1, CH - scalar_cols(i + 1), CH, scopy)
-                jw = i // 2 + 1
-                if jw < 16:
-                    widen(jw, (0, 1) if i % 2 == 0 else (2, 3))
+                if i + 2 - i % 2 < STEPS:
+                    widen(i + 2 - i % 2, (0, 1) if i % 2 == 0 else (2, 3))
                 if i in (11, 19):
                     unturn(scopy, "n%d" % i, new_group, 0 if i == 11 else 2)
                 if 29 <= i < STEPS - 1:

@@ -19,8 +19,8 @@ P = 128
 PACK = 4
 PASS = P * PACK
 CH = 512
-PAIR = 2 * CH
-STEPS = 32
+GROUPS = [(0, 1), (1, 1)] + [(i, 2) for i in range(2, 30, 2)] + [(30, 1), (31, 1)]
+LAST = len(GROUPS) - 1
 
 
 def tile_legendrememoryunitstep_w_kernel(tc, z, m, ez, at, bvec, wz_bytes, wz_scale, wm, out):
@@ -30,7 +30,8 @@ def tile_legendrememoryunitstep_w_kernel(tc, z, m, ez, at, bvec, wz_bytes, wz_sc
         raw_pool = ctx.enter_context(tc.tile_pool(name="raw", bufs=4))
         wide_pool = ctx.enter_context(tc.tile_pool(name="wide", bufs=3))
         group_pool = ctx.enter_context(tc.tile_pool(name="group", bufs=3))
-        code_pool = ctx.enter_context(tc.tile_pool(name="code", bufs=7))
+        code_pool = ctx.enter_context(tc.tile_pool(name="code", bufs=4))
+        res_pool = ctx.enter_context(tc.tile_pool(name="res", bufs=2))
         acc_pool = ctx.enter_context(tc.psum_pool(name="acc", bufs=1))
         turn_pool = ctx.enter_context(tc.psum_pool(name="turn", bufs=2))
 
@@ -46,15 +47,13 @@ def tile_legendrememoryunitstep_w_kernel(tc, z, m, ez, at, bvec, wz_bytes, wz_sc
         ez_sb = keep.tile([P, 8, PACK], BF16, name="ez_sb")
         bvec_sb = keep.tile([P, MEM], BF16, name="bvec_sb")
         z_sb = keep.tile([P, K], BF16, name="z_sb", align_bytes=64)
-        m_sb = keep.tile([P, MEM], BF16, name="m_sb", align_bytes=64)
+        m_sb = keep.tile([P, MEM], BF16, name="mem_rows", align_bytes=64)
         z_group = keep.tile([P, 8, PASS], BF16, name="z_group", align_bytes=64)
         z_codes = keep.tile([P, 8, TOK], U32, name="z_codes", align_bytes=64)
         z_scales = keep.tile([P, 8, TOK], U8, name="z_scales", align_bytes=64)
-        m_group = keep.tile([P, 4, PASS], BF16, name="m_group", align_bytes=64)
+        m_group = keep.tile([P, 4, PASS], BF16, name="mem_group", align_bytes=64)
         m_codes = keep.tile([P, 4, TOK], U32, name="m_codes", align_bytes=64)
         m_scales = keep.tile([P, 4, TOK], U8, name="m_scales", align_bytes=64)
-        new_sb = keep.tile([P, MEM], BF16, name="new_sb", align_bytes=64)
-        new_group = keep.tile([P, 4, PASS], BF16, name="new_group", align_bytes=64)
         new_codes = keep.tile([P, 4, TOK], U32, name="new_codes", align_bytes=64)
         new_scales = keep.tile([P, 4, TOK], U8, name="new_scales", align_bytes=64)
         u_sb = keep.tile([P, 1], F32, name="u_sb")
@@ -62,110 +61,99 @@ def tile_legendrememoryunitstep_w_kernel(tc, z, m, ez, at, bvec, wz_bytes, wz_sc
 
         scale_view = wz_scale.rearrange("(g p t) o -> p g (t o)", p=P, t=PACK)
         ez_view = ez.rearrange("(g p t) -> p g t", p=P, t=PACK)
-        at_view = at.rearrange("(g p t) n -> g p t n", p=P, t=PACK)
-        wm_view = wm.rearrange("(g p t) n -> g p t n", p=P, t=PACK)
+        plain_view = [w.rearrange("(g p t) n -> g p t n", p=P, t=PACK) for w in (at, wm)]
         wz_view = wz_bytes.rearrange("(g p t) n -> g p t n", p=P, t=PACK)
 
         acc = [acc_pool.tile([P, CH], F32, name="acc%d" % c) for c in range(4)]
+        vcopy = nc.vector.tensor_copy
+        scopy = nc.scalar.copy
 
         def plain_unit(i):
             r = i % 16
             return i // 16, (r % 8) // 2, 2 * (r // 8) + r % 2
 
-        vcopy = nc.vector.tensor_copy
-        scopy = nc.scalar.copy
+        raw, raw_z, wide, woven, group_b, group_z, codes_b, codes_z = {}, {}, {}, {}, {}, {}, {}, {}
+        first, turned, mem = {}, {}, {}
 
-        woven = {}
-        raw = {}
-        codes_raw = {}
-        wide = {}
-        group_b = {}
-        group_z = {}
-        codes_b = {}
-        codes_z = {}
-        first = {}
-
-        def load_plain(i, n=2):
+        def load_plain(q):
+            i, n = GROUPS[q]
             which, g, c = plain_unit(i)
-            pool = raw_pool if n == 2 else keep
-            t = pool.tile([P, PACK, n * CH], BF16, name="raw_b" if n == 2 else "raw_b%d" % i, align_bytes=64)
-            for k in range(n):
-                raw[i + k] = (t, k * CH)
-            nc.sync.dma_start(out=t[:], in_=(at_view, wm_view)[which][g][:, :, c * CH : (c + n) * CH])
+            parts = 2 if q == 0 else 1
+            w = n * CH // parts
+            raw[q] = []
+            for k in range(parts):
+                t = (keep if q == 0 else raw_pool).tile(
+                    [P, PACK, w], BF16, name="raw_b0%d" % k if q == 0 else "raw_b", align_bytes=64
+                )
+                raw[q].append(t)
+                lo = c * CH + k * w
+                nc.sync.dma_start(out=t[:], in_=plain_view[which][g][:, :, lo : lo + w])
 
-        def load_bytes(i, n=2):
+        def load_bytes(q):
+            i, n = GROUPS[q]
             g, c = i // 4, i % 4
-            pool = raw_pool if n == 2 else keep
-            t = pool.tile([P, PACK, n * CH], U8, name="raw_z" if n == 2 else "raw_z%d" % i, align_bytes=64)
-            for k in range(n):
-                codes_raw[i + k] = (t, k * CH)
+            t = raw_pool.tile([P, PACK, n * CH], U8, name="raw_z", align_bytes=64)
+            raw_z[q] = t
             nc.sync.dma_start(out=t[:], in_=wz_view[g][:, :, c * CH : (c + n) * CH])
 
         def scale_col(g, t):
             return scale_first[:, t : t + 1] if g == 0 else scale_rest[:, g - 1, t : t + 1]
 
-        def widen(i, ts, n=2):
-            if i not in wide:
-                pool = wide_pool if n == 2 else keep
-                wt = pool.tile([P, PACK, n * CH], BF16, name="wide" if n == 2 else "wide%d" % i, align_bytes=64)
-                for k in range(n):
-                    wide[i + k] = (wt, k * CH)
-            for t in ts:
+        def widen(q):
+            i, n = GROUPS[q]
+            wt = wide_pool.tile([P, PACK, n * CH], BF16, name="wide", align_bytes=64)
+            wide[q] = [wt]
+            for t in range(PACK):
                 nc.scalar.activation(
-                    out=wide[i][0][:, t, :],
-                    in_=codes_raw[i][0][:, t, :].bitcast(FP8),
-                    func=ACT.Copy,
-                    scale=scale_col(i // 4, t),
+                    out=wt[:, t, :], in_=raw_z[q][:, t, :].bitcast(FP8), func=ACT.Copy, scale=scale_col(i // 4, t)
                 )
 
-        def interleave(engine_copy, dst, source, a, b):
-            src, off = source
-            engine_copy(
-                out=dst[:, a:b, :].rearrange("p (c i) t -> p c t i", i=4),
-                in_=src[:, :, off + a : off + b].rearrange("p t (c i) -> p c t i", i=4),
-            )
+        def interleave(copy, store, source, q, a, b, name):
+            if b <= a:
+                return
+            if q not in store:
+                gt = group_pool.tile([P, GROUPS[q][1] * CH, PACK], BF16, name=name, align_bytes=64)
+                store[q] = gt
+            w = (b - a) // len(source[q])
+            for k, src in enumerate(source[q]):
+                lo = a if len(source[q]) == 1 else 0
+                copy(
+                    out=store[q][:, a + k * w : a + (k + 1) * w, :].rearrange("p (c i) t -> p c t i", i=4),
+                    in_=src[:, :, lo : lo + w].rearrange("p t (c i) -> p c t i", i=4),
+                )
 
-        def get_group(store, i, name):
-            if i not in store:
-                gt = group_pool.tile([P, CH, PACK], BF16, name=name, align_bytes=64)
-                store[i] = gt
-            return store[i]
+        def share_b(copy, q, a, b):
+            interleave(copy, group_b, raw, q, a, b, "group_b")
 
-        def share_b(i, a, b, engine_copy):
-            if b > a:
-                interleave(engine_copy, get_group(group_b, i, "group_b"), raw[i], a, b)
+        def share_z(copy, q, a, b):
+            interleave(copy, group_z, wide, q, a, b, "group_z")
 
-        def share_z(i, a, b, engine_copy):
-            if b > a:
-                interleave(engine_copy, get_group(group_z, i, "group_z"), wide[i], a, b)
-
-        def tensor_share_b(i):
-            src, off = raw[i]
+        def tensor_share(q):
             it = turn_pool.tile([P, 2, CH], BF16, name="turned")
-            woven[i] = it
+            woven[q] = it
             for k in (0, 1):
-                lo = off + CH // 2 + k * P
+                lo = 6 * P + k * P
                 nc.tensor.matmul(
                     it[:, k, :],
                     lhsT=ident_b[:],
-                    rhs=src[:, :, lo : lo + P].rearrange("p t c -> p c t"),
+                    rhs=raw[q][0][:, :, lo : lo + P].rearrange("p t c -> p c t"),
                     start=True,
                     stop=True,
                 )
 
-        def fetch_share_b(i):
+        def fetch_tensor_share(q):
             nc.scalar.copy(
-                out=get_group(group_b, i, "group_b")[:, CH // 2 :, :].rearrange("p c t -> p (c t)"),
-                in_=woven[i][:].rearrange("p k n -> p (k n)"),
+                out=group_b[q][:, 6 * P :, :].rearrange("p c t -> p (c t)"),
+                in_=woven[q][:].rearrange("p k n -> p (k n)"),
             )
 
-
-        def quantize(store, groups, i, name):
-            ct = code_pool.tile([P, CH], U32, name="codes_" + name, align_bytes=64)
-            st = code_pool.tile([P, CH], U8, name="scales_" + name, align_bytes=64)
-            store[i] = (ct, st)
+        def quantize(store, groups, q, name):
+            w = GROUPS[q][1] * CH
+            ct = code_pool.tile([P, w], U32, name="codes_" + name, align_bytes=64)
+            st = code_pool.tile([P, w], U8, name="scales_" + name, align_bytes=64)
+            store[q] = (ct, st)
             nc.vector.quantize_mx(
-                out=ct[:].bitcast(FP8X4), scales=st[:], in_=groups[i][:].rearrange("p w j -> p (w j)")
+                out=ct[:].bitcast(FP8X4), scales=st[:], in_=groups[q][:].rearrange("p w j -> p (w j)")
             )
 
         def quantize_rows(codes, scales, group, g0, g1):
@@ -175,33 +163,35 @@ def tile_legendrememoryunitstep_w_kernel(tc, z, m, ez, at, bvec, wz_bytes, wz_sc
                 in_=group[:, g0:g1, :].rearrange("p g k -> p (g k)"),
             )
 
-        def mm(acc_ap, codes, scales, g, pair, start, stop):
+        def mm(acc_ap, codes, scales, g, pair, k, start, stop):
             ct, st = pair
             nc.tensor.matmul_mx(
                 out=acc_ap,
                 lhsT=codes[:, g, :].bitcast(FP8X4),
                 lhsT_scale=scales[:, g, :],
-                rhs=ct[:].bitcast(FP8X4),
-                rhs_scale=st[:],
+                rhs=ct[:, k * CH : (k + 1) * CH].bitcast(FP8X4),
+                rhs_scale=st[:, k * CH : (k + 1) * CH],
                 start=start,
                 stop=stop,
             )
 
-        def mm_b(i):
-            which, g, c = plain_unit(i)
-            if which == 0:
-                if g == 0:
-                    ft = acc_pool.tile([P, CH], F32, name="first%d" % (c % 2))
-                    first[c] = ft
-                mm(first[c][:], m_codes, m_scales, g, codes_b[i], g == 0, g == 3)
-            else:
-                mm(acc[c][:], new_codes, new_scales, g, codes_b[i], False, False)
+        def mm_b(q):
+            i, n = GROUPS[q]
+            for k in range(n):
+                which, g, c = plain_unit(i + k)
+                if which == 0:
+                    if g == 0:
+                        ft = acc_pool.tile([P, CH], F32, name="first%d" % (c % 2))
+                        first[c] = ft
+                    mm(first[c][:], m_codes, m_scales, g, codes_b[q], k, g == 0, g == 3)
+                else:
+                    mm(acc[c][:], new_codes, new_scales, g, codes_b[q], k, False, False)
 
-        def mm_z(i):
-            g, c = i // 4, i % 4
-            mm(acc[c][:], z_codes, z_scales, g, codes_z[i], g == 0, g == 7)
-
-        turned = {}
+        def mm_z(q):
+            i, n = GROUPS[q]
+            for k in range(n):
+                g, c = (i + k) // 4, (i + k) % 4
+                mm(acc[c][:], z_codes, z_scales, g, codes_z[q], k, g == 0, g == 7)
 
         def turn(key, src, g):
             tt = turn_pool.tile([P, 2, 2, TOK], F32, name="turned")
@@ -218,9 +208,9 @@ def tile_legendrememoryunitstep_w_kernel(tc, z, m, ez, at, bvec, wz_bytes, wz_sc
                 in_=turned[key][:].rearrange("p g u r -> p g r u"),
             )
 
-        def turn_z(q):
-            turn("z%d" % q, z_sb, 2 * q)
-            unturn(vcopy, "z%d" % q, z_group, 2 * q)
+        def turn_z(r):
+            turn("z%d" % r, z_sb, 2 * r)
+            unturn(vcopy, "z%d" % r, z_group, 2 * r)
 
         def write_scalar(u_ps):
             for g in range(8):
@@ -233,14 +223,14 @@ def tile_legendrememoryunitstep_w_kernel(tc, z, m, ez, at, bvec, wz_bytes, wz_sc
                         stop=(g == 7 and t == PACK - 1),
                     )
 
-        def finish(c):
-            res = keep.tile([P, CH], F32, name="res%d" % c)
-            nc.scalar.activation(out=res[:], in_=acc[c][:], func=ACT.Tanh)
-            nc.sync.dma_start(out=out[:, c * CH : (c + 1) * CH], in_=res[:])
+        def finish(c, a=0, b=CH, queue=nc.sync):
+            res = res_pool.tile([P, b - a], F32, name="res")
+            nc.scalar.activation(out=res[:], in_=acc[c][:, a:b], func=ACT.Tanh)
+            queue.dma_start(out=out[:, c * CH + a : c * CH + b], in_=res[:])
 
         def add_write(c):
             nc.vector.scalar_tensor_tensor(
-                out=new_sb[:, c * CH : (c + 1) * CH],
+                out=mem["new"][:, c * CH : (c + 1) * CH],
                 in0=bvec_sb[:, c * CH : (c + 1) * CH],
                 scalar=u_sb[:, 0:1],
                 in1=first[c][:],
@@ -248,101 +238,115 @@ def tile_legendrememoryunitstep_w_kernel(tc, z, m, ez, at, bvec, wz_bytes, wz_sc
                 op1=ALU.add,
             )
 
-        def scalar_cols(i):
-            if i < 3:
-                return 0
-            if i == 3:
-                return 128
-            return 256 if i in by_tensor else 240
+        woven_groups = range(4, 16)
 
-        by_tensor = range(6, 29, 2)
+        def split_b(q):
+            w = GROUPS[q][1] * CH
+            if q < 3:
+                return w, w
+            if q == 3:
+                return w - 400, w
+            if q in woven_groups:
+                return 6 * P - 272, 6 * P
+            return w - 192, w
 
-        def scalar_cols_z(i):
-            return 160 if i >= 30 else 0
+        def split_z(q):
+            w = GROUPS[q][1] * CH
+            return w - (192 if q == LAST else 0)
 
+        def scalar_part(q):
+            if q > LAST:
+                return
+            widen(q)
+            a, b = split_b(q)
+            share_b(scopy, q, a, b)
+            if q in woven_groups:
+                fetch_tensor_share(q)
+            share_z(scopy, q, split_z(q), GROUPS[q][1] * CH)
 
         with tc.manual_schedule():
             nc.scalar.dma_start(out=scale_first[:], in_=scale_view[:, 0, :])
             nc.scalar.activation(out=warm[:], in_=zero[:], func=ACT.Tanh)
-            load_bytes(0, 1)
-            load_plain(0, 1)
-            load_bytes(1, 1)
+            load_bytes(0)
+            load_plain(0)
+            load_bytes(1)
             nc.sync.dma_start(out=m_sb[:], in_=m)
-            load_plain(1, 1)
+            load_plain(1)
             nc.sync.dma_start(out=z_sb[:, 0 : K // 2], in_=z[:, 0 : K // 2])
             nc.sync.dma_start(out=z_sb[:, K // 2 : K], in_=z[:, K // 2 : K])
             nc.scalar.dma_start(out=scale_rest[:], in_=scale_view[:, 1:8, :])
             nc.scalar.dma_start(out=ez_sb[:], in_=ez_view)
-            load_bytes(2)
-            load_plain(2)
-            load_bytes(4)
-            load_plain(4)
+            for q in (2, 3):
+                load_bytes(q)
+                load_plain(q)
             nc.sync.dma_start(out=bvec_sb[:], in_=bvec.partition_broadcast(P))
-            load_bytes(6)
 
-            widen(0, range(4), 1)
-            turn("m0", m_sb, 0)
-            turn("m1", m_sb, 2)
-            unturn(scopy, "m0", m_group, 0)
-            unturn(scopy, "m1", m_group, 2)
-            widen(1, range(4), 1)
+            scalar_part(0)
+            for g in (0, 2):
+                turn("m%d" % g, m_sb, g)
+            for g in (0, 2):
+                unturn(scopy, "m%d" % g, m_group, g)
+            scalar_part(1)
 
-            for i in range(STEPS):
-                if i % 2 == 0:
-                    if i + 6 < STEPS:
-                        load_plain(i + 6)
-                    if i + 8 < STEPS:
-                        load_bytes(i + 8)
+            for q in range(LAST + 1):
+                if q >= 1 and q + 3 <= LAST:
+                    load_plain(q + 3)
+                if q + 4 <= LAST:
+                    load_bytes(q + 4)
 
-                if i + 2 in by_tensor:
-                    tensor_share_b(i + 2)
-                if i + 1 in by_tensor:
-                    fetch_share_b(i + 1)
-                elif i + 1 < STEPS:
-                    share_b(i + 1, CH - scalar_cols(i + 1), CH, scopy)
-                if i + 2 - i % 2 < STEPS:
-                    widen(i + 2 - i % 2, (0, 1) if i % 2 == 0 else (2, 3))
-                if i in (11, 19):
-                    unturn(scopy, "n%d" % i, new_group, 0 if i == 11 else 2)
-                if 29 <= i < STEPS - 1:
-                    share_z(i + 1, CH - scalar_cols_z(i + 1), CH, scopy)
+                if q + 2 in woven_groups:
+                    tensor_share(q + 2)
+                if q == 0:
+                    scalar_part(2)
+                elif q >= 1:
+                    scalar_part(q + 2) if q + 2 < 4 else None
+                    scalar_part(q + 1) if q + 1 >= 4 else None
+                if q in (6, 10):
+                    unturn(scopy, "n%d" % (q - 1), mem["group"], 0 if q == 6 else 2)
 
-                share_b(i, 0, CH - scalar_cols(i), vcopy)
-                if i == 1:
+                share_b(vcopy, q, 0, split_b(q)[0])
+                if q == 1:
                     turn_z(0)
                     turn_z(1)
-                if i == 2:
                     quantize_rows(m_codes, m_scales, m_group, 0, 4)
-                if i == 3:
+                if q == 2:
                     quantize_rows(z_codes, z_scales, z_group, 0, 4)
-                if i == 4:
-                    quantize_rows(z_codes, z_scales, z_group, 4, 8)
                     vcopy(out=u_sb[:], in_=u_ps[:])
-                if i in (12, 20):
-                    quantize_rows(new_codes, new_scales, new_group, (i - 12) // 4, (i - 12) // 4 + 2)
-                if i > 0:
-                    quantize(codes_z, group_z, i - 1, "z")
-                if i in (8, 9, 16, 17):
-                    add_write((0, 1, 2, 3)[(8, 9, 16, 17).index(i)])
-                share_z(i, 0, CH - scalar_cols_z(i), vcopy)
-                if i == 1:
+                if q in (7, 11):
+                    quantize_rows(new_codes, new_scales, mem["group"], (q - 7) // 2, (q - 7) // 2 + 2)
+                if q > 0:
+                    quantize(codes_z, group_z, q - 1, "z")
+                if q in (5, 9):
+                    if q == 5:
+                        new_sb = keep.tile([P, MEM], BF16, name="mem_rows", align_bytes=64)
+                        new_group = keep.tile([P, 4, PASS], BF16, name="mem_group", align_bytes=64)
+                        mem["new"], mem["group"] = new_sb, new_group
+                    add_write((q - 5) // 2)
+                    add_write((q - 5) // 2 + 1)
+                share_z(vcopy, q, 0, split_z(q))
+                if q == 1:
                     turn_z(2)
                     turn_z(3)
                     u_ps = turn_pool.tile([P, 1], F32, name="turned")
                     write_scalar(u_ps)
-                quantize(codes_b, group_b, i, "b")
-                if i == STEPS - 1:
-                    quantize(codes_z, group_z, i, "z")
+                if q == 2:
+                    quantize_rows(z_codes, z_scales, z_group, 4, 8)
+                quantize(codes_b, group_b, q, "b")
+                if q == LAST:
+                    quantize(codes_z, group_z, q, "z")
 
-                if i in (10, 18):
-                    turn("n%d" % (i + 1), new_sb, 0 if i == 10 else 2)
-                if i >= 4:
-                    for k in range(5) if i == 4 else (i,):
+                if q >= 2:
+                    for k in range(3) if q == 2 else (q,):
                         if k > 0:
                             mm_z(k - 1)
+                        if k in (5, 9):
+                            turn("n%d" % k, mem["new"], 0 if k == 5 else 2)
                         mm_b(k)
-                if i == STEPS - 1:
-                    mm_z(i)
-                if i >= 29:
-                    finish(i - 29)
-            finish(3)
+                if q == LAST:
+                    mm_z(q)
+                if q == LAST - 1:
+                    finish(0)
+                    finish(1)
+            finish(2)
+            finish(3, 0, CH // 2)
+            finish(3, CH // 2, CH, nc.scalar)

from contextlib import ExitStack

import concourse.mybir as mybir
from concourse.masks import make_identity

TOK, K, MEM, H = 128, 4096, 2048, 2048
FLOPS = 2 * TOK * (MEM * MEM + K * H + MEM * H + K + MEM)

F32 = mybir.dt.float32
BF16 = mybir.dt.bfloat16
U32 = mybir.dt.uint32
U8 = mybir.dt.uint8
FP8 = mybir.dt.float8_e4m3fn
FP8X4 = mybir.dt.float8_e4m3fn_x4
ACT = mybir.ActivationFunctionType
ALU = mybir.AluOpType

P = 128
PACK = 4
PASS = P * PACK
CH = 512
GROUPS = [(0, 1), (1, 1)] + [(i, 2) for i in range(2, 30, 2)] + [(30, 1), (31, 1)]
LAST = len(GROUPS) - 1


def tile_legendrememoryunitstep_w_kernel(tc, z, m, ez, at, bvec, wz_bytes, wz_scale, wm, out):
    nc = tc.nc
    with ExitStack() as ctx:
        keep = ctx.enter_context(tc.tile_pool(name="keep", bufs=1))
        raw_pool = ctx.enter_context(tc.tile_pool(name="raw", bufs=4))
        wide_pool = ctx.enter_context(tc.tile_pool(name="wide", bufs=3))
        group_pool = ctx.enter_context(tc.tile_pool(name="group", bufs=3))
        code_pool = ctx.enter_context(tc.tile_pool(name="code", bufs=4))
        res_pool = ctx.enter_context(tc.tile_pool(name="res", bufs=2))
        acc_pool = ctx.enter_context(tc.psum_pool(name="acc", bufs=1))
        turn_pool = ctx.enter_context(tc.psum_pool(name="turn", bufs=2))

        ident = keep.tile([P, P], F32, name="ident")
        make_identity(nc, ident[:])
        ident_b = keep.tile([P, P], BF16, name="ident_b")
        nc.vector.tensor_copy(out=ident_b[:], in_=ident[:])
        zero = keep.tile([P, 1], F32, name="zero")
        nc.vector.memset(zero[:], 0.0)

        scale_first = keep.tile([P, PACK], F32, name="scale_first")
        scale_rest = keep.tile([P, 7, PACK], F32, name="scale_rest")
        ez_sb = keep.tile([P, 8, PACK], BF16, name="ez_sb")
        bvec_sb = keep.tile([P, MEM], BF16, name="bvec_sb")
        z_sb = keep.tile([P, K], BF16, name="z_sb", align_bytes=64)
        m_sb = keep.tile([P, MEM], BF16, name="mem_rows", align_bytes=64)
        z_group = keep.tile([P, 8, PASS], BF16, name="z_group", align_bytes=64)
        z_codes = keep.tile([P, 8, TOK], U32, name="z_codes", align_bytes=64)
        z_scales = keep.tile([P, 8, TOK], U8, name="z_scales", align_bytes=64)
        m_group = keep.tile([P, 4, PASS], BF16, name="mem_group", align_bytes=64)
        m_codes = keep.tile([P, 4, TOK], U32, name="m_codes", align_bytes=64)
        m_scales = keep.tile([P, 4, TOK], U8, name="m_scales", align_bytes=64)
        new_codes = keep.tile([P, 4, TOK], U32, name="new_codes", align_bytes=64)
        new_scales = keep.tile([P, 4, TOK], U8, name="new_scales", align_bytes=64)
        u_sb = keep.tile([P, 1], F32, name="u_sb")
        warm = keep.tile([P, 1], F32, name="warm")

        scale_view = wz_scale.rearrange("(g p t) o -> p g (t o)", p=P, t=PACK)
        ez_view = ez.rearrange("(g p t) -> p g t", p=P, t=PACK)
        plain_view = [w.rearrange("(g p t) n -> g p t n", p=P, t=PACK) for w in (at, wm)]
        wz_view = wz_bytes.rearrange("(g p t) n -> g p t n", p=P, t=PACK)

        acc = [acc_pool.tile([P, CH], F32, name="acc%d" % c) for c in range(4)]
        vcopy = nc.vector.tensor_copy
        scopy = nc.scalar.copy

        def plain_unit(i):
            r = i % 16
            return i // 16, (r % 8) // 2, 2 * (r // 8) + r % 2

        raw, raw_z, wide, woven, group_b, group_z, codes_b, codes_z = {}, {}, {}, {}, {}, {}, {}, {}
        first, turned, mem = {}, {}, {}

        def load_plain(q):
            i, n = GROUPS[q]
            which, g, c = plain_unit(i)
            parts = 2 if q == 0 else 1
            w = n * CH // parts
            raw[q] = []
            for k in range(parts):
                t = (keep if q == 0 else raw_pool).tile(
                    [P, PACK, w], BF16, name="raw_b0%d" % k if q == 0 else "raw_b", align_bytes=64
                )
                raw[q].append(t)
                lo = c * CH + k * w
                nc.sync.dma_start(out=t[:], in_=plain_view[which][g][:, :, lo : lo + w])

        def load_bytes(q):
            i, n = GROUPS[q]
            g, c = i // 4, i % 4
            t = raw_pool.tile([P, PACK, n * CH], U8, name="raw_z", align_bytes=64)
            raw_z[q] = t
            nc.sync.dma_start(out=t[:], in_=wz_view[g][:, :, c * CH : (c + n) * CH])

        def scale_col(g, t):
            return scale_first[:, t : t + 1] if g == 0 else scale_rest[:, g - 1, t : t + 1]

        def widen(q):
            i, n = GROUPS[q]
            wt = wide_pool.tile([P, PACK, n * CH], BF16, name="wide", align_bytes=64)
            wide[q] = [wt]
            for t in range(PACK):
                nc.scalar.activation(
                    out=wt[:, t, :], in_=raw_z[q][:, t, :].bitcast(FP8), func=ACT.Copy, scale=scale_col(i // 4, t)
                )

        def interleave(copy, store, source, q, a, b, name):
            if b <= a:
                return
            if q not in store:
                gt = group_pool.tile([P, GROUPS[q][1] * CH, PACK], BF16, name=name, align_bytes=64)
                store[q] = gt
            w = (b - a) // len(source[q])
            for k, src in enumerate(source[q]):
                lo = a if len(source[q]) == 1 else 0
                copy(
                    out=store[q][:, a + k * w : a + (k + 1) * w, :].rearrange("p (c i) t -> p c t i", i=4),
                    in_=src[:, :, lo : lo + w].rearrange("p t (c i) -> p c t i", i=4),
                )

        def share_b(copy, q, a, b):
            interleave(copy, group_b, raw, q, a, b, "group_b")

        def share_z(copy, q, a, b):
            interleave(copy, group_z, wide, q, a, b, "group_z")

        def tensor_share(q):
            it = turn_pool.tile([P, 2, CH], BF16, name="turned")
            woven[q] = it
            for k in (0, 1):
                lo = 6 * P + k * P
                nc.tensor.matmul(
                    it[:, k, :],
                    lhsT=ident_b[:],
                    rhs=raw[q][0][:, :, lo : lo + P].rearrange("p t c -> p c t"),
                    start=True,
                    stop=True,
                )

        def fetch_tensor_share(q):
            nc.scalar.copy(
                out=group_b[q][:, 6 * P :, :].rearrange("p c t -> p (c t)"),
                in_=woven[q][:].rearrange("p k n -> p (k n)"),
            )

        def quantize(store, groups, q, name):
            w = GROUPS[q][1] * CH
            ct = code_pool.tile([P, w], U32, name="codes_" + name, align_bytes=64)
            st = code_pool.tile([P, w], U8, name="scales_" + name, align_bytes=64)
            store[q] = (ct, st)
            nc.vector.quantize_mx(
                out=ct[:].bitcast(FP8X4), scales=st[:], in_=groups[q][:].rearrange("p w j -> p (w j)")
            )

        def quantize_rows(codes, scales, group, g0, g1):
            nc.vector.quantize_mx(
                out=codes[:, g0:g1, :].rearrange("p g n -> p (g n)").bitcast(FP8X4),
                scales=scales[:, g0:g1, :].rearrange("p g n -> p (g n)"),
                in_=group[:, g0:g1, :].rearrange("p g k -> p (g k)"),
            )

        def mm(acc_ap, codes, scales, g, pair, k, start, stop):
            ct, st = pair
            nc.tensor.matmul_mx(
                out=acc_ap,
                lhsT=codes[:, g, :].bitcast(FP8X4),
                lhsT_scale=scales[:, g, :],
                rhs=ct[:, k * CH : (k + 1) * CH].bitcast(FP8X4),
                rhs_scale=st[:, k * CH : (k + 1) * CH],
                start=start,
                stop=stop,
            )

        def mm_b(q):
            i, n = GROUPS[q]
            for k in range(n):
                which, g, c = plain_unit(i + k)
                if which == 0:
                    if g == 0:
                        ft = acc_pool.tile([P, CH], F32, name="first%d" % (c % 2))
                        first[c] = ft
                    mm(first[c][:], m_codes, m_scales, g, codes_b[q], k, g == 0, g == 3)
                else:
                    mm(acc[c][:], new_codes, new_scales, g, codes_b[q], k, False, False)

        def mm_z(q):
            i, n = GROUPS[q]
            for k in range(n):
                g, c = (i + k) // 4, (i + k) % 4
                mm(acc[c][:], z_codes, z_scales, g, codes_z[q], k, g == 0, g == 7)

        def turn(key, src, g):
            tt = turn_pool.tile([P, 2, 2, TOK], F32, name="turned")
            turned[key] = tt
            words = src[:].bitcast(F32)
            for k in (0, 1):
                for u in (0, 1):
                    lo = 256 * (g + k)
                    nc.tensor.transpose(tt[:, k, u, :], words[:, lo + u : lo + 256 : 2], ident[:])

        def unturn(copy, key, group, g):
            copy(
                out=group[:, g : g + 2, :].bitcast(F32).rearrange("p g (r u) -> p g r u", u=2),
                in_=turned[key][:].rearrange("p g u r -> p g r u"),
            )

        def turn_z(r):
            turn("z%d" % r, z_sb, 2 * r)
            unturn(vcopy, "z%d" % r, z_group, 2 * r)

        def write_scalar(u_ps):
            for g in range(8):
                for t in range(PACK):
                    nc.tensor.matmul(
                        u_ps[:],
                        lhsT=z_group[:, g, :].rearrange("p (n t) -> p n t", t=PACK)[:, :, t],
                        rhs=ez_sb[:, g, t : t + 1],
                        start=(g == 0 and t == 0),
                        stop=(g == 7 and t == PACK - 1),
                    )

        def finish(c, a=0, b=CH, queue=nc.sync):
            res = res_pool.tile([P, b - a], F32, name="res")
            nc.scalar.activation(out=res[:], in_=acc[c][:, a:b], func=ACT.Tanh)
            queue.dma_start(out=out[:, c * CH + a : c * CH + b], in_=res[:])

        def add_write(c):
            nc.vector.scalar_tensor_tensor(
                out=mem["new"][:, c * CH : (c + 1) * CH],
                in0=bvec_sb[:, c * CH : (c + 1) * CH],
                scalar=u_sb[:, 0:1],
                in1=first[c][:],
                op0=ALU.mult,
                op1=ALU.add,
            )

        woven_groups = range(4, 16)

        def split_b(q):
            w = GROUPS[q][1] * CH
            if q < 3:
                return w, w
            if q == 3:
                return w - 400, w
            if q in woven_groups:
                return 6 * P - 272, 6 * P
            return w - 192, w

        def split_z(q):
            w = GROUPS[q][1] * CH
            return w - (192 if q == LAST else 0)

        def scalar_part(q):
            if q > LAST:
                return
            widen(q)
            a, b = split_b(q)
            share_b(scopy, q, a, b)
            if q in woven_groups:
                fetch_tensor_share(q)
            share_z(scopy, q, split_z(q), GROUPS[q][1] * CH)

        with tc.manual_schedule():
            nc.scalar.dma_start(out=scale_first[:], in_=scale_view[:, 0, :])
            nc.scalar.activation(out=warm[:], in_=zero[:], func=ACT.Tanh)
            load_bytes(0)
            load_plain(0)
            load_bytes(1)
            nc.sync.dma_start(out=m_sb[:], in_=m)
            load_plain(1)
            nc.sync.dma_start(out=z_sb[:, 0 : K // 2], in_=z[:, 0 : K // 2])
            nc.sync.dma_start(out=z_sb[:, K // 2 : K], in_=z[:, K // 2 : K])
            nc.scalar.dma_start(out=scale_rest[:], in_=scale_view[:, 1:8, :])
            nc.scalar.dma_start(out=ez_sb[:], in_=ez_view)
            for q in (2, 3):
                load_bytes(q)
                load_plain(q)
            nc.sync.dma_start(out=bvec_sb[:], in_=bvec.partition_broadcast(P))

            scalar_part(0)
            for g in (0, 2):
                turn("m%d" % g, m_sb, g)
            for g in (0, 2):
                unturn(scopy, "m%d" % g, m_group, g)
            scalar_part(1)

            for q in range(LAST + 1):
                if q >= 1 and q + 3 <= LAST:
                    load_plain(q + 3)
                if q + 4 <= LAST:
                    load_bytes(q + 4)

                if q + 2 in woven_groups:
                    tensor_share(q + 2)
                if q == 0:
                    scalar_part(2)
                elif q >= 1:
                    scalar_part(q + 2) if q + 2 < 4 else None
                    scalar_part(q + 1) if q + 1 >= 4 else None
                if q in (6, 10):
                    unturn(scopy, "n%d" % (q - 1), mem["group"], 0 if q == 6 else 2)

                share_b(vcopy, q, 0, split_b(q)[0])
                if q == 1:
                    turn_z(0)
                    turn_z(1)
                    quantize_rows(m_codes, m_scales, m_group, 0, 4)
                if q == 2:
                    quantize_rows(z_codes, z_scales, z_group, 0, 4)
                    vcopy(out=u_sb[:], in_=u_ps[:])
                if q in (7, 11):
                    quantize_rows(new_codes, new_scales, mem["group"], (q - 7) // 2, (q - 7) // 2 + 2)
                if q > 0:
                    quantize(codes_z, group_z, q - 1, "z")
                if q in (5, 9):
                    if q == 5:
                        new_sb = keep.tile([P, MEM], BF16, name="mem_rows", align_bytes=64)
                        new_group = keep.tile([P, 4, PASS], BF16, name="mem_group", align_bytes=64)
                        mem["new"], mem["group"] = new_sb, new_group
                    add_write((q - 5) // 2)
                    add_write((q - 5) // 2 + 1)
                share_z(vcopy, q, 0, split_z(q))
                if q == 1:
                    turn_z(2)
                    turn_z(3)
                    u_ps = turn_pool.tile([P, 1], F32, name="turned")
                    write_scalar(u_ps)
                if q == 2:
                    quantize_rows(z_codes, z_scales, z_group, 4, 8)
                quantize(codes_b, group_b, q, "b")
                if q == LAST:
                    quantize(codes_z, group_z, q, "z")

                if q >= 2:
                    for k in range(3) if q == 2 else (q,):
                        if k > 0:
                            mm_z(k - 1)
                        if k in (5, 9):
                            turn("n%d" % k, mem["new"], 0 if k == 5 else 2)
                        mm_b(k)
                if q == LAST:
                    mm_z(q)
                if q == LAST - 1:
                    finish(0)
                    finish(1)
            finish(2)
            finish(3, 0, CH // 2)
            finish(3, CH // 2, CH, nc.scalar)
